import numpy as np
import ml_dtypes

BF16 = ml_dtypes.bfloat16


def bf(x):
    return np.asarray(x, np.float32).astype(BF16)


def f32(x):
    return np.asarray(x, np.float32)


def f64(x):
    return np.asarray(x).astype(np.float64)


def striped(idx):
    return np.concatenate([l.reshape(-1, 16).T for l in idx])


def rows(idx, k):
    return np.tile(np.repeat(idx, 16, axis=0), (k // (16 * 8), 1))


def look(tab, idx):
    return np.take_along_axis(f64(tab), rows(idx, len(tab)), axis=1)


K, S, V, N, M = 256, 2048, 1024, 1024, 256


def angles():
    a = np.random.uniform(0.0, 2.0 * np.pi, (K, S))
    return np.stack([np.cos(a), np.sin(a)])


def setup_inputs():
    return {"tab": f32(angles()), "x0": f32(np.random.standard_normal((K, V))), "x1": f32(np.random.standard_normal((K, V))), "w": bf(np.random.standard_normal((K, M)) / np.sqrt(K)), "b": f32(0.5 * np.random.standard_normal((M, 1))), "offs": striped(np.random.randint(0, S, (8, N)))}


def reference(tab, x0, x1, w, b, offs):
    idx = np.stack([g.T.reshape(-1) for g in np.split(offs, 8)])
    x = f64(x0) * look(tab[0], idx) + f64(x1) * look(tab[1], idx)
    y = f64(w).T @ x
    return np.maximum(y + f64(b), 0.0)

@@ -1,0 +1,63 @@
+import concourse.mybir as mybir
+
+F32, BF16, U16 = mybir.dt.float32, mybir.dt.bfloat16, mybir.dt.uint16
+MULT, ADD = mybir.AluOpType.mult, mybir.AluOpType.add
+RELU = mybir.ActivationFunctionType.Relu
+
+P = 128
+GROUP = 16
+PIECE = 512
+K, N, M = 256, 1024, 256
+FLOPS = 2 * K * M * N
+
+
+def tile_lookup_rope_mul_relu_kernel(tc, tab, x0, x1, w, b, offs, out):
+    nc = tc.nc
+    positions = tab.shape[2]
+    blocks, halves, pieces = K // P, M // P, N // PIECE
+    with (
+        tc.tile_pool(name="held", bufs=1) as held,
+        tc.psum_pool(name="psum", bufs=1) as psum,
+    ):
+        offsets = held.tile([P, N // GROUP], U16, name="offsets")
+        nc.sync.dma_start(offsets[:], offs)
+
+        bias = held.tile([P, halves], F32, name="bias")
+        nc.scalar.dma_start(bias[:], b.rearrange("(p h) o -> p (h o)", h=halves))
+        weights = held.tile([P, blocks, M], BF16, name="weights")
+        nc.scalar.dma_start(weights[:], w.rearrange("(k p) m -> p k m", p=P))
+
+        windows, values = {}, {}
+        for k in range(blocks):
+            rows = slice(k * P, (k + 1) * P)
+            for t, source in enumerate((x0, x1)):
+                windows[k, t] = held.tile([P, positions], F32, name=f"window{k}{t}")
+                nc.sync.dma_start(windows[k, t][:], tab[t, rows, :])
+                for c in range(pieces):
+                    values[k, t, c] = held.tile([P, PIECE], F32, name=f"values{k}{t}{c}")
+                    nc.sync.dma_start(values[k, t, c][:], source[rows, c * PIECE:(c + 1) * PIECE])
+
+        banks = {(c, h): psum.tile([P, PIECE], F32, name=f"bank{c}{h}")
+                 for c in range(pieces) for h in range(halves)}
+        out_by_half = out.rearrange("(p h) n -> p h n", h=halves)
+
+        for k in range(blocks):
+            products = {}
+            for t in range(2):
+                for c in range(pieces):
+                    entries = offsets[:, c * PIECE // GROUP:(c + 1) * PIECE // GROUP]
+                    products[t, c] = held.tile([P, PIECE], F32, name=f"product{k}{t}{c}")
+                    nc.vector.tensor_tensor(products[t, c][:], windows[k, t][:].indirect(entries),
+                                            values[k, t, c][:], MULT)
+            for c in range(pieces):
+                rotated = held.tile([P, PIECE], BF16, name=f"rotated{k}{c}")
+                nc.vector.tensor_tensor(rotated[:], products[0, c][:], products[1, c][:], ADD)
+                for h in range(halves):
+                    nc.tensor.matmul(banks[c, h][:], weights[:, k, h::halves], rotated[:],
+                                     start=(k == 0), stop=(k == blocks - 1))
+
+        for c in range(pieces):
+            for h in range(halves):
+                result = held.tile([P, PIECE], F32, name=f"result{c}{h}")
+                nc.scalar.activation(result[:], banks[c, h][:], RELU, bias=bias[:, h:h + 1])
+                nc.sync.dma_start(out_by_half[:, h, c * PIECE:(c + 1) * PIECE], result[:])

@@ -1,12 +1,12 @@
 import concourse.mybir as mybir
 
 F32, BF16, U16 = mybir.dt.float32, mybir.dt.bfloat16, mybir.dt.uint16
-MULT, ADD = mybir.AluOpType.mult, mybir.AluOpType.add
+MULT, ADD, MAX = mybir.AluOpType.mult, mybir.AluOpType.add, mybir.AluOpType.max
 RELU = mybir.ActivationFunctionType.Relu
 
 P = 128
 GROUP = 16
-PIECE = 512
+PIECE = 256
 K, N, M = 256, 1024, 256
 FLOPS = 2 * K * M * N
 
@@ -15,49 +15,77 @@ def tile_lookup_rope_mul_relu_kernel(tc, tab, x0, x1, w, b, offs, out):
     nc = tc.nc
     positions = tab.shape[2]
     blocks, halves, pieces = K // P, M // P, N // PIECE
+
+    def columns(c, count=1):
+        return slice(c * PIECE, (c + count) * PIECE)
+
     with (
         tc.tile_pool(name="held", bufs=1) as held,
         tc.psum_pool(name="psum", bufs=1) as psum,
     ):
-        offsets = held.tile([P, N // GROUP], U16, name="offsets")
-        nc.sync.dma_start(offsets[:], offs)
-
         bias = held.tile([P, halves], F32, name="bias")
         nc.scalar.dma_start(bias[:], b.rearrange("(p h) o -> p (h o)", h=halves))
-        weights = held.tile([P, blocks, M], BF16, name="weights")
-        nc.scalar.dma_start(weights[:], w.rearrange("(k p) m -> p k m", p=P))
+        out_by_half = out.rearrange("(p h) n -> p h n", h=halves)
 
+        offsets = held.tile([P, N // GROUP], U16, name="offsets")
+        weights = held.tile([P, blocks, M], BF16, name="weights")
         windows, values = {}, {}
         for k in range(blocks):
             rows = slice(k * P, (k + 1) * P)
             for t, source in enumerate((x0, x1)):
                 windows[k, t] = held.tile([P, positions], F32, name=f"window{k}{t}")
+                values[k, t] = held.tile([P, N], F32, name=f"values{k}{t}")
                 nc.sync.dma_start(windows[k, t][:], tab[t, rows, :])
-                for c in range(pieces):
-                    values[k, t, c] = held.tile([P, PIECE], F32, name=f"values{k}{t}{c}")
-                    nc.sync.dma_start(values[k, t, c][:], source[rows, c * PIECE:(c + 1) * PIECE])
+                if (k, t) == (0, 0):
+                    nc.sync.dma_start(offsets[:], offs)
+                for part in (columns(0), columns(1), columns(2, 2)):
+                    nc.sync.dma_start(values[k, t][:, part], source[rows, part])
+            if k == 0:
+                nc.sync.dma_start(weights[:], w.rearrange("(k p) m -> p k m", p=P))
+        last_weights = held.tile([P, M], F32, name="last_weights")
+        nc.scalar.copy(last_weights[:], weights[:, blocks - 1, :])
 
         banks = {(c, h): psum.tile([P, PIECE], F32, name=f"bank{c}{h}")
                  for c in range(pieces) for h in range(halves)}
-        out_by_half = out.rearrange("(p h) n -> p h n", h=halves)
 
         for k in range(blocks):
-            products = {}
-            for t in range(2):
-                for c in range(pieces):
-                    entries = offsets[:, c * PIECE // GROUP:(c + 1) * PIECE // GROUP]
-                    products[t, c] = held.tile([P, PIECE], F32, name=f"product{k}{t}{c}")
-                    nc.vector.tensor_tensor(products[t, c][:], windows[k, t][:].indirect(entries),
-                                            values[k, t, c][:], MULT)
+            last = k == blocks - 1
+            products = [held.tile([P, N], F32, name=f"product{k}{t}") for t in range(2)]
+            rotated = held.tile([P, N], BF16, name=f"rotated{k}")
+
+            def summed_by_matmul(c):
+                return last and c == 0
+
+            def gather_product(t, c):
+                entries = offsets[:, c * PIECE // GROUP:(c + 1) * PIECE // GROUP]
+                nc.vector.tensor_tensor(products[t][:, columns(c)], windows[k, t][:].indirect(entries),
+                                        values[k, t][:, columns(c)], MULT)
+                if summed_by_matmul(c):
+                    for h in range(halves):
+                        nc.tensor.matmul(banks[c, h][:], last_weights[:, h::halves], products[t][:, columns(c)],
+                                         start=False, stop=(t == 1))
+
+            def add_and_multiply(c):
+                if not summed_by_matmul(c):
+                    nc.vector.tensor_tensor(rotated[:, columns(c)], products[0][:, columns(c)],
+                                            products[1][:, columns(c)], ADD)
+                    for h in range(halves):
+                        nc.tensor.matmul(banks[c, h][:], weights[:, k, h::halves], rotated[:, columns(c)],
+                                         start=(k == 0), stop=last)
+
             for c in range(pieces):
-                rotated = held.tile([P, PIECE], BF16, name=f"rotated{k}{c}")
-                nc.vector.tensor_tensor(rotated[:], products[0, c][:], products[1, c][:], ADD)
-                for h in range(halves):
-                    nc.tensor.matmul(banks[c, h][:], weights[:, k, h::halves], rotated[:],
-                                     start=(k == 0), stop=(k == blocks - 1))
+                gather_product(0, c)
+            for c in range(pieces):
+                gather_product(1, c)
+                if c > 0:
+                    add_and_multiply(c - 1)
+            add_and_multiply(pieces - 1)
 
         for c in range(pieces):
             for h in range(halves):
                 result = held.tile([P, PIECE], F32, name=f"result{c}{h}")
-                nc.scalar.activation(result[:], banks[c, h][:], RELU, bias=bias[:, h:h + 1])
-                nc.sync.dma_start(out_by_half[:, h, c * PIECE:(c + 1) * PIECE], result[:])
+                if h == 1 and c >= pieces - 2:
+                    nc.vector.tensor_scalar(result[:], banks[c, h][:], bias[:, h:h + 1], 0.0, ADD, MAX)
+                else:
+                    nc.scalar.activation(result[:], banks[c, h][:], RELU, bias=bias[:, h:h + 1])
+                nc.sync.dma_start(out_by_half[:, h, columns(c)], result[:])

@@ -38,10 +38,11 @@ def tile_lookup_rope_mul_relu_kernel(tc, tab, x0, x1, w, b, offs, out):
                 nc.sync.dma_start(windows[k, t][:], tab[t, rows, :])
                 if (k, t) == (0, 0):
                     nc.sync.dma_start(offsets[:], offs)
-                for part in (columns(0), columns(1), columns(2, 2)):
+                parts = (columns(0), columns(1), columns(2, 2)) if t == 1 else (columns(0, pieces),)
+                for part in parts:
                     nc.sync.dma_start(values[k, t][:, part], source[rows, part])
-            if k == 0:
-                nc.sync.dma_start(weights[:], w.rearrange("(k p) m -> p k m", p=P))
+                if (k, t) == (blocks - 1, 0):
+                    nc.sync.dma_start(weights[:], w.rearrange("(k p) m -> p k m", p=P))
         last_weights = held.tile([P, M], F32, name="last_weights")
         nc.scalar.copy(last_weights[:], weights[:, blocks - 1, :])
 

@@ -6,27 +6,22 @@ RELU = mybir.ActivationFunctionType.Relu
 
 P = 128
 GROUP = 16
-PIECE = 256
 K, N, M = 256, 1024, 256
+WIDTHS = (320, 320, 192, 192)
 FLOPS = 2 * K * M * N
 
 
 def tile_lookup_rope_mul_relu_kernel(tc, tab, x0, x1, w, b, offs, out):
     nc = tc.nc
     positions = tab.shape[2]
-    blocks, halves, pieces = K // P, M // P, N // PIECE
-
-    def columns(c, count=1):
-        return slice(c * PIECE, (c + count) * PIECE)
+    blocks, halves = K // P, M // P
+    pieces = [slice(sum(WIDTHS[:c]), sum(WIDTHS[:c + 1])) for c in range(len(WIDTHS))]
+    final = len(pieces) - 1
 
     with (
         tc.tile_pool(name="held", bufs=1) as held,
         tc.psum_pool(name="psum", bufs=1) as psum,
     ):
-        bias = held.tile([P, halves], F32, name="bias")
-        nc.scalar.dma_start(bias[:], b.rearrange("(p h) o -> p (h o)", h=halves))
-        out_by_half = out.rearrange("(p h) n -> p h n", h=halves)
-
         offsets = held.tile([P, N // GROUP], U16, name="offsets")
         weights = held.tile([P, blocks, M], BF16, name="weights")
         windows, values = {}, {}
@@ -38,7 +33,7 @@ def tile_lookup_rope_mul_relu_kernel(tc, tab, x0, x1, w, b, offs, out):
                 nc.sync.dma_start(windows[k, t][:], tab[t, rows, :])
                 if (k, t) == (0, 0):
                     nc.sync.dma_start(offsets[:], offs)
-                parts = (columns(0), columns(1), columns(2, 2)) if t == 1 else (columns(0, pieces),)
+                parts = (pieces[0], pieces[1], slice(pieces[2].start, N)) if t == 1 else (slice(0, N),)
                 for part in parts:
                     nc.sync.dma_start(values[k, t][:, part], source[rows, part])
                 if (k, t) == (blocks - 1, 0):
@@ -46,8 +41,12 @@ def tile_lookup_rope_mul_relu_kernel(tc, tab, x0, x1, w, b, offs, out):
         last_weights = held.tile([P, M], F32, name="last_weights")
         nc.scalar.copy(last_weights[:], weights[:, blocks - 1, :])
 
-        banks = {(c, h): psum.tile([P, PIECE], F32, name=f"bank{c}{h}")
-                 for c in range(pieces) for h in range(halves)}
+        bias = held.tile([P, halves], F32, name="bias")
+        nc.sync.dma_start(bias[:], b.rearrange("(p h) o -> p (h o)", h=halves))
+        out_by_half = out.rearrange("(p h) n -> p h n", h=halves)
+
+        banks = {(c, h): psum.tile([P, width], F32, name=f"bank{c}{h}")
+                 for c, width in enumerate(WIDTHS) for h in range(halves)}
 
         for k in range(blocks):
             last = k == blocks - 1
@@ -58,35 +57,35 @@ def tile_lookup_rope_mul_relu_kernel(tc, tab, x0, x1, w, b, offs, out):
                 return last and c == 0
 
             def gather_product(t, c):
-                entries = offsets[:, c * PIECE // GROUP:(c + 1) * PIECE // GROUP]
-                nc.vector.tensor_tensor(products[t][:, columns(c)], windows[k, t][:].indirect(entries),
-                                        values[k, t][:, columns(c)], MULT)
+                entries = offsets[:, pieces[c].start // GROUP:pieces[c].stop // GROUP]
+                nc.vector.tensor_tensor(products[t][:, pieces[c]], windows[k, t][:].indirect(entries),
+                                        values[k, t][:, pieces[c]], MULT)
                 if summed_by_matmul(c):
                     for h in range(halves):
-                        nc.tensor.matmul(banks[c, h][:], last_weights[:, h::halves], products[t][:, columns(c)],
+                        nc.tensor.matmul(banks[c, h][:], last_weights[:, h::halves], products[t][:, pieces[c]],
                                          start=False, stop=(t == 1))
 
             def add_and_multiply(c):
                 if not summed_by_matmul(c):
-                    nc.vector.tensor_tensor(rotated[:, columns(c)], products[0][:, columns(c)],
-                                            products[1][:, columns(c)], ADD)
+                    nc.vector.tensor_tensor(rotated[:, pieces[c]], products[0][:, pieces[c]],
+                                            products[1][:, pieces[c]], ADD)
                     for h in range(halves):
-                        nc.tensor.matmul(banks[c, h][:], weights[:, k, h::halves], rotated[:, columns(c)],
+                        nc.tensor.matmul(banks[c, h][:], weights[:, k, h::halves], rotated[:, pieces[c]],
                                          start=(k == 0), stop=last)
 
-            for c in range(pieces):
+            for c in range(len(pieces)):
                 gather_product(0, c)
-            for c in range(pieces):
+            for c in range(len(pieces)):
                 gather_product(1, c)
                 if c > 0:
                     add_and_multiply(c - 1)
-            add_and_multiply(pieces - 1)
+            add_and_multiply(final)
 
-        for c in range(pieces):
+        for c, width in enumerate(WIDTHS):
             for h in range(halves):
-                result = held.tile([P, PIECE], F32, name=f"result{c}{h}")
-                if h == 1 and c >= pieces - 2:
+                result = held.tile([P, width], F32, name=f"result{c}{h}")
+                if h == 1 and c >= final - 1:
                     nc.vector.tensor_scalar(result[:], banks[c, h][:], bias[:, h:h + 1], 0.0, ADD, MAX)
                 else:
                     nc.scalar.activation(result[:], banks[c, h][:], RELU, bias=bias[:, h:h + 1])
-                nc.sync.dma_start(out_by_half[:, h, columns(c)], result[:])
+                nc.sync.dma_start(out_by_half[:, h, pieces[c]], result[:])

import concourse.mybir as mybir

F32, BF16, U16 = mybir.dt.float32, mybir.dt.bfloat16, mybir.dt.uint16
MULT, ADD, MAX = mybir.AluOpType.mult, mybir.AluOpType.add, mybir.AluOpType.max
RELU = mybir.ActivationFunctionType.Relu

P = 128
GROUP = 16
K, N, M = 256, 1024, 256
WIDTHS = (320, 320, 192, 192)
FLOPS = 2 * K * M * N


def tile_lookup_rope_mul_relu_kernel(tc, tab, x0, x1, w, b, offs, out):
    nc = tc.nc
    positions = tab.shape[2]
    blocks, halves = K // P, M // P
    pieces = [slice(sum(WIDTHS[:c]), sum(WIDTHS[:c + 1])) for c in range(len(WIDTHS))]
    final = len(pieces) - 1

    with (
        tc.tile_pool(name="held", bufs=1) as held,
        tc.psum_pool(name="psum", bufs=1) as psum,
    ):
        offsets = held.tile([P, N // GROUP], U16, name="offsets")
        weights = held.tile([P, blocks, M], BF16, name="weights")
        windows, values = {}, {}
        for k in range(blocks):
            rows = slice(k * P, (k + 1) * P)
            for t, source in enumerate((x0, x1)):
                windows[k, t] = held.tile([P, positions], F32, name=f"window{k}{t}")
                values[k, t] = held.tile([P, N], F32, name=f"values{k}{t}")
                nc.sync.dma_start(windows[k, t][:], tab[t, rows, :])
                if (k, t) == (0, 0):
                    nc.sync.dma_start(offsets[:], offs)
                parts = (pieces[0], pieces[1], slice(pieces[2].start, N)) if t == 1 else (slice(0, N),)
                for part in parts:
                    nc.sync.dma_start(values[k, t][:, part], source[rows, part])
                if (k, t) == (blocks - 1, 0):
                    nc.sync.dma_start(weights[:], w.rearrange("(k p) m -> p k m", p=P))
        last_weights = held.tile([P, M], F32, name="last_weights")
        nc.scalar.copy(last_weights[:], weights[:, blocks - 1, :])

        bias = held.tile([P, halves], F32, name="bias")
        nc.sync.dma_start(bias[:], b.rearrange("(p h) o -> p (h o)", h=halves))
        out_by_half = out.rearrange("(p h) n -> p h n", h=halves)

        banks = {(c, h): psum.tile([P, width], F32, name=f"bank{c}{h}")
                 for c, width in enumerate(WIDTHS) for h in range(halves)}

        for k in range(blocks):
            last = k == blocks - 1
            products = [held.tile([P, N], F32, name=f"product{k}{t}") for t in range(2)]
            rotated = held.tile([P, N], BF16, name=f"rotated{k}")

            def summed_by_matmul(c):
                return last and c == 0

            def gather_product(t, c):
                entries = offsets[:, pieces[c].start // GROUP:pieces[c].stop // GROUP]
                nc.vector.tensor_tensor(products[t][:, pieces[c]], windows[k, t][:].indirect(entries),
                                        values[k, t][:, pieces[c]], MULT)
                if summed_by_matmul(c):
                    for h in range(halves):
                        nc.tensor.matmul(banks[c, h][:], last_weights[:, h::halves], products[t][:, pieces[c]],
                                         start=False, stop=(t == 1))

            def add_and_multiply(c):
                if not summed_by_matmul(c):
                    nc.vector.tensor_tensor(rotated[:, pieces[c]], products[0][:, pieces[c]],
                                            products[1][:, pieces[c]], ADD)
                    for h in range(halves):
                        nc.tensor.matmul(banks[c, h][:], weights[:, k, h::halves], rotated[:, pieces[c]],
                                         start=(k == 0), stop=last)

            for c in range(len(pieces)):
                gather_product(0, c)
            for c in range(len(pieces)):
                gather_product(1, c)
                if c > 0:
                    add_and_multiply(c - 1)
            add_and_multiply(final)

        for c, width in enumerate(WIDTHS):
            for h in range(halves):
                result = held.tile([P, width], F32, name=f"result{c}{h}")
                if h == 1 and c >= final - 1:
                    nc.vector.tensor_scalar(result[:], banks[c, h][:], bias[:, h:h + 1], 0.0, ADD, MAX)
                else:
                    nc.scalar.activation(result[:], banks[c, h][:], RELU, bias=bias[:, h:h + 1])
                nc.sync.dma_start(out_by_half[:, h, pieces[c]], result[:])
